import numpy as np
CORES = [2,42,66,74,82,90,114]
N = 7
T, W, CAP = 256, 64, 128
def entries(a): return a.T.reshape(-1)
def pack(v, P): return np.ascontiguousarray(np.asarray(v, np.int32).reshape(-1, P).T)
def lists(rng, how):
    L = rng.integers(0, T, (N, N, CAP))
    if how == "alike": L[:] = rng.integers(0, T, (N, N, 1))
    if how == "distinct": L = np.stack([np.stack([rng.permutation(T)[:CAP] for d in range(N)]) for r in range(N)])
    if how == "sorted": L = np.sort(L, axis=2)
    if how == "edge": L = np.where(rng.random((N, N, CAP)) < 0.5, 0, T - 1)
    return {"l": np.stack([pack(L[r].reshape(-1), 128) for r in range(N)])}
def setup_inputs(rng):
    return dict({"x": rng.standard_normal((N, T, W), dtype=np.float32)}, **lists(rng, "uniform"))
def setup_inputs_alike(rng):
    d = setup_inputs(rng); d.update(lists(rng, "alike"))
    for k in ("x",): d[k] = (d[k].astype(np.float32) * 1048576.0).astype(d[k].dtype)
    return d
def setup_inputs_distinct(rng):
    d = setup_inputs(rng); d.update(lists(rng, "distinct"))
    for k in ("x",): d[k] = (d[k].astype(np.float32) * (1 / 1024.0)).astype(d[k].dtype)
    return d
def setup_inputs_edge(rng):
    d = setup_inputs(rng); d.update(lists(rng, "edge"))
    return d
def setup_inputs_sorted(rng):
    d = setup_inputs(rng); d.update(lists(rng, "sorted"))
    return d
def check_inputs(x):
    bad = []
    if x["l"].min() < 0 or x["l"].max() >= T: bad.append("l out of range")
    return bad
def reference(x, l):
    y = np.zeros((N, N * CAP, W), x.dtype)
    for r in range(N):
        L = entries(l[r])
        for d in range(N): y[d][CAP * r:CAP * r + CAP] = x[r][L[CAP * d:CAP * d + CAP]]
    return {"y": y}

@@ -1,0 +1,143 @@
+from concourse.bass import DstId, RemoteDMATransfer
+from concourse.mybir import AluOpType
+
+N = 7
+CAP = 128
+W = 64
+NB = 4
+
+SCRATCH = {
+    "li": ("sbuf", [128, N], "int32"),
+    "lf": ("sbuf", [128, N], "float32"),
+    "xs": ("sbuf", [128, 2 * W], "float32"),
+    "tt": ("sbuf", [128, 128], "int32"),
+    "m1": ("sbuf", [128, 8], "int32"),
+    "msk": ("sbuf", [128, 8], "float32"),
+    "s1": ("sbuf", [128, 128], "int32"),
+    "sel": ("sbuf", [128, 128], "bfloat16"),
+    "ident": ("sbuf", [128, 128], "float32"),
+    "rr": ("sbuf", [128, 8 * N], "bfloat16"),
+    "off": ("sbuf", [128, 8 * N], "uint16"),
+    "win": ("sbuf", [128, 256], "float32"),
+    "gat": ("sbuf", [128, N * CAP], "float32"),
+    "snd": ("sbuf", [128, N * W], "float32"),
+    "land": ("dram", [N, 128, W], "float32"),
+    "pxa": ("psum", [128, 512], "float32"),
+    "pxb": ("psum", [128, 512], "float32"),
+    "po": ("psum", [128, 512], "float32"),
+    "pb0": ("psum", [128, 512], "float32"),
+    "pb1": ("psum", [128, 512], "float32"),
+    "pb2": ("psum", [128, 512], "float32"),
+    "pb3": ("psum", [128, 512], "float32"),
+}
+SEMAPHORES = (["l_in", "x_in", "c_t", "c_win", "c_m1", "c_id", "c_s1", "c_msk", "c_sel", "c_lf", "c_rr", "c_w", "c_off",
+               "p_t0", "p_t1", "p_off", "sent", "st"]
+              + ["gk%d" % k for k in range(N)] + ["bk%d" % k for k in range(N)] + ["ck%d" % k for k in range(N)]
+              + ["a%d" % k for k in range(N)])
+
+
+def engines(m):
+    return [e for e in range(m.bit_length()) if (m >> e) & 1]
+
+
+def rank_program(g, core, T, topo):
+    rank = T.rank_of(core)
+    if rank is None:
+        return
+    V, PE, SY, SC, sem = g.vector, g.tensor, g.sync, g.scalar, T.sem
+    steps = (N - 1) // 2
+    up = [(rank + 1 + s) % N for s in range(steps)]
+    down = [(rank - 1 - s) % N for s in range(steps)]
+    order = []
+    for s in range(steps):
+        order += [up[s], down[s]]
+    order.append(rank)
+
+    SY.dma_start(T.li[:, :], T.l[:, :]).then_inc(sem.l_in, 16)
+    SC.dma_start(T.xs[:, :], T.x[:, :]).then_inc(sem.x_in, 16)
+
+    g.iota(T.tt[:, :], [[-1, 128]], 128, 1).then_inc(sem.c_t, 1)
+    V.memset(T.win[64:128, :], 0.0).then_inc(sem.c_win, 1)
+    V.wait_ge(sem.c_t, 1)
+    V.tensor_scalar(T.m1[:, :], T.tt[:, 0:128:16], 4, None, AluOpType.arith_shift_right).then_inc(sem.c_m1, 1)
+    V.tensor_scalar(T.ident[:, :], T.tt[:, :], 128, None, AluOpType.is_equal).then_inc(sem.c_id, 1)
+    V.tensor_scalar(T.s1[:, :], T.tt[:, :], 15, None, AluOpType.bitwise_and).then_inc(sem.c_s1, 1)
+    V.wait_ge(sem.c_m1, 1)
+    V.tensor_scalar(T.msk[:, :], T.m1[:, :], 8, None, AluOpType.is_equal).then_inc(sem.c_msk, 1)
+    V.wait_ge(sem.c_s1, 1)
+    V.tensor_scalar(T.sel[:, :], T.s1[:, :], 0, None, AluOpType.is_equal).then_inc(sem.c_sel, 1)
+
+    V.wait_ge(sem.l_in, 16)
+    V.tensor_copy(T.lf[:, :], T.li[:, :]).then_inc(sem.c_lf, 1)
+    V.wait_ge(sem.c_lf, 1)
+    V.wait_ge(sem.c_msk, 1)
+    for k, d in enumerate(order):
+        V.tensor_scalar(T.rr[:, 8 * k:8 * k + 8], T.msk[:, :], T.lf[:, d:d + 1], None,
+                        AluOpType.mult).then_inc(sem.c_rr, 1)
+
+    PE.wait_ge(sem.x_in, 16)
+    PE.wait_ge(sem.c_id, 1)
+    PE.transpose(T.pxa[0:W, 0:128], T.xs[:, 0:W], T.ident[:, :]).then_inc(sem.p_t0, 1)
+    PE.transpose(T.pxb[0:W, 0:128], T.xs[:, W:2 * W], T.ident[:, :]).then_inc(sem.p_t1, 1)
+    PE.wait_ge(sem.c_rr, N)
+    PE.wait_ge(sem.c_sel, 1)
+    PE.matmul(T.po[:, 0:8 * N], T.sel[:, :], T.rr[:, :], True, True).then_inc(sem.p_off, 1)
+
+    V.wait_ge(sem.p_t0, 1)
+    V.tensor_copy(T.win[0:W, 0:256:2], T.pxa[0:W, 0:128]).then_inc(sem.c_w, 1)
+    V.wait_ge(sem.p_t1, 1)
+    V.tensor_copy(T.win[0:W, 1:256:2], T.pxb[0:W, 0:128]).then_inc(sem.c_w, 1)
+    V.wait_ge(sem.p_off, 1)
+    V.tensor_copy(T.off[:, :], T.po[:, 0:8 * N]).then_inc(sem.c_off, 1)
+    V.wait_ge(sem.c_w, 2)
+    V.wait_ge(sem.c_off, 1)
+    V.wait_ge(sem.c_win, 1)
+
+    def gather(k):
+        V.tensor_copy(T.gat[:, CAP * k:CAP * (k + 1)],
+                      T.win[:, 0:256].indirect(T.off[:, 8 * k:8 * k + 8])).then_inc(sem["gk%d" % k], 1)
+
+    gather(0)
+    gather(1)
+    for k in range(N):
+        bank = T["pb%d" % (k % NB)]
+        PE.wait_ge(sem["gk%d" % k], 1)
+        if k >= NB:
+            PE.wait_ge(sem["ck%d" % (k - NB)], 1)
+        PE.transpose(bank[:, 0:W], T.gat[0:W, CAP * k:CAP * (k + 1)], T.ident[0:W, 0:W]).then_inc(sem["bk%d" % k], 1)
+        V.wait_ge(sem["bk%d" % k], 1)
+        V.tensor_copy(T.snd[:, W * k:W * (k + 1)], bank[:, 0:W]).then_inc(sem["ck%d" % k], 1)
+        if k + 2 < N:
+            gather(k + 2)
+
+    sent = 0
+    for s in range(steps):
+        pair = [order[2 * s], order[2 * s + 1]]
+        for d in pair:
+            if not topo.may_write(core, T.cores[d]):
+                raise ValueError("core %d may not write to core %d" % (core, T.cores[d]))
+        eng = engines(topo.mask(core, T.cores[pair[0]]) & topo.mask(core, T.cores[pair[1]]))
+        half = len(eng) // 2
+        trs = []
+        for i, d in enumerate(pair):
+            rid, pid, _se = topo.addr(T.cores[d])
+            k = 2 * s + i
+            g.wait_ge(sem["ck%d" % k], 1)
+            trs.append(RemoteDMATransfer(dst_ids=[DstId(rid=rid, pnc=pid)],
+                                         dma_engine_mask=sum(1 << e for e in eng[i * half:(i + 1) * half]),
+                                         remote_sem=sem["a%d" % rank],
+                                         src=T.snd[:, W * k:W * (k + 1)], dst=T.land[rank]))
+            sent += half
+        g.remote_dma_fused(trs, local_sem=sem.sent)
+
+    SY.wait_ge(sem["ck%d" % (N - 1)], 1)
+    SY.dma_start(T.y[CAP * rank:CAP * (rank + 1), :], T.snd[:, W * (N - 1):W * N]).then_inc(sem.st, 16)
+    for s in range(steps):
+        for q, src in ((SY, down[s]), (SC, up[s])):
+            other = (2 * src - rank) % N
+            n = len(engines(topo.mask(T.cores[src], core) & topo.mask(T.cores[src], T.cores[other]))) // 2
+            q.wait_ge(sem["a%d" % src], n)
+            q.dma_start(T.y[CAP * src:CAP * (src + 1), :], T.land[src]).then_inc(sem.st, 16)
+
+    g.wait_ge(sem.sent, sent)
+    g.wait_ge(sem.st, 16 * N)

@@ -1,24 +1,29 @@
 from concourse.bass import DstId, RemoteDMATransfer
-from concourse.mybir import AluOpType
+from concourse.mybir import AluOpType, ActivationFunctionType
 
 N = 7
 CAP = 128
 W = 64
 NB = 4
+NJ = N - 1
+XW = 2 * W + N
 
 SCRATCH = {
     "li": ("sbuf", [128, N], "int32"),
-    "lf": ("sbuf", [128, N], "float32"),
-    "xs": ("sbuf", [128, 2 * W], "float32"),
+    "xs": ("sbuf", [128, XW], "float32"),
+    "fx": ("sbuf", [128, XW], "float32"),
     "tt": ("sbuf", [128, 128], "int32"),
     "m1": ("sbuf", [128, 8], "int32"),
     "msk": ("sbuf", [128, 8], "float32"),
     "s1": ("sbuf", [128, 128], "int32"),
     "sel": ("sbuf", [128, 128], "bfloat16"),
     "ident": ("sbuf", [128, 128], "float32"),
-    "rr": ("sbuf", [128, 8 * N], "bfloat16"),
-    "off": ("sbuf", [128, 8 * N], "uint16"),
+    "rr": ("sbuf", [128, 8 * NJ], "bfloat16"),
+    "rr2": ("sbuf", [128, 8], "bfloat16"),
+    "off": ("sbuf", [128, 8 * NJ], "uint16"),
+    "off2": ("sbuf", [128, 8], "uint16"),
     "win": ("sbuf", [128, 256], "float32"),
+    "win2": ("sbuf", [128, 256], "float32"),
     "gat": ("sbuf", [128, N * CAP], "float32"),
     "snd": ("sbuf", [128, N * W], "float32"),
     "land": ("dram", [N, 128, W], "float32"),
@@ -30,14 +35,28 @@ SCRATCH = {
     "pb2": ("psum", [128, 512], "float32"),
     "pb3": ("psum", [128, 512], "float32"),
 }
-SEMAPHORES = (["l_in", "x_in", "c_t", "c_win", "c_m1", "c_id", "c_s1", "c_msk", "c_sel", "c_lf", "c_rr", "c_w", "c_off",
-               "p_t0", "p_t1", "p_off", "sent", "st"]
+SEMAPHORES = (["l_in", "x_in", "c_t", "c_win", "c_win2", "c_m1", "c_id", "c_s1", "c_msk", "c_sel", "c_lf", "c_rr",
+               "c_w0", "c_w1", "c_off", "p_t0", "p_t1", "p_off", "sent", "st",
+               "fa", "f_rr", "f_t0", "f_t1", "f_po", "f_w0", "f_w1", "f_off"]
               + ["gk%d" % k for k in range(N)] + ["bk%d" % k for k in range(N)] + ["ck%d" % k for k in range(N)]
               + ["a%d" % k for k in range(N)])
+
+CALLS = [[2, -2], [3, -3], [-1]]
+RAW = 1
 
 
 def engines(m):
     return [e for e in range(m.bit_length()) if (m >> e) & 1]
+
+
+def shares(topo, cores, src, call):
+    m = None
+    for sh in call:
+        mm = topo.mask(cores[src], cores[(src + sh) % N])
+        m = mm if m is None else (m & mm)
+    eng = engines(m)
+    part = len(eng) // len(call)
+    return [eng[i * part:(i + 1) * part] for i in range(len(call))]
 
 
 def rank_program(g, core, T, topo):
@@ -45,99 +64,145 @@ def rank_program(g, core, T, topo):
     if rank is None:
         return
     V, PE, SY, SC, sem = g.vector, g.tensor, g.sync, g.scalar, T.sem
-    steps = (N - 1) // 2
-    up = [(rank + 1 + s) % N for s in range(steps)]
-    down = [(rank - 1 - s) % N for s in range(steps)]
-    order = []
-    for s in range(steps):
-        order += [up[s], down[s]]
-    order.append(rank)
+    cores = T.cores
+    order = [(rank + sh) % N for call in CALLS for sh in call] + [rank]
+    raw_dst, raw_src = (rank + RAW) % N, (rank - RAW) % N
+    for d in order[:-1] + [raw_dst]:
+        if not topo.may_write(core, cores[d]):
+            raise ValueError("core %d may not write to core %d" % (core, cores[d]))
+
+    def copy(q, out, in_):
+        if q is V:
+            return V.tensor_copy(out, in_)
+        return SC.activation(out, in_, ActivationFunctionType.Copy)
 
     SY.dma_start(T.li[:, :], T.l[:, :]).then_inc(sem.l_in, 16)
-    SC.dma_start(T.xs[:, :], T.x[:, :]).then_inc(sem.x_in, 16)
+    SC.dma_start(T.xs[:, 0:2 * W], T.x[:, :]).then_inc(sem.x_in, 16)
 
     g.iota(T.tt[:, :], [[-1, 128]], 128, 1).then_inc(sem.c_t, 1)
     V.memset(T.win[64:128, :], 0.0).then_inc(sem.c_win, 1)
     V.wait_ge(sem.c_t, 1)
-    V.tensor_scalar(T.m1[:, :], T.tt[:, 0:128:16], 4, None, AluOpType.arith_shift_right).then_inc(sem.c_m1, 1)
     V.tensor_scalar(T.ident[:, :], T.tt[:, :], 128, None, AluOpType.is_equal).then_inc(sem.c_id, 1)
-    V.tensor_scalar(T.s1[:, :], T.tt[:, :], 15, None, AluOpType.bitwise_and).then_inc(sem.c_s1, 1)
+    V.tensor_scalar(T.m1[:, :], T.tt[:, 0:128:16], 4, None, AluOpType.arith_shift_right).then_inc(sem.c_m1, 1)
     V.wait_ge(sem.c_m1, 1)
     V.tensor_scalar(T.msk[:, :], T.m1[:, :], 8, None, AluOpType.is_equal).then_inc(sem.c_msk, 1)
+    V.wait_ge(sem.l_in, 16)
+    V.tensor_copy(T.xs[:, 2 * W:XW], T.li[:, :]).then_inc(sem.c_lf, 1)
+
+    sent = 0
+    raw_eng = shares(topo, cores, rank, [RAW])[0]
+    rid, pid, _se = topo.addr(cores[raw_dst])
+    g.wait_ge(sem.x_in, 16)
+    g.wait_ge(sem.c_lf, 1)
+    g.remote_dma_fused([RemoteDMATransfer(dst_ids=[DstId(rid=rid, pnc=pid)],
+                                          dma_engine_mask=sum(1 << e for e in raw_eng), remote_sem=sem.fa,
+                                          src=T.xs[:, :], dst=T.fx[:, :])], local_sem=sem.sent)
+    sent += len(raw_eng)
+
+    V.tensor_scalar(T.s1[:, :], T.tt[:, :], 15, None, AluOpType.bitwise_and).then_inc(sem.c_s1, 1)
     V.wait_ge(sem.c_s1, 1)
     V.tensor_scalar(T.sel[:, :], T.s1[:, :], 0, None, AluOpType.is_equal).then_inc(sem.c_sel, 1)
-
-    V.wait_ge(sem.l_in, 16)
-    V.tensor_copy(T.lf[:, :], T.li[:, :]).then_inc(sem.c_lf, 1)
     V.wait_ge(sem.c_lf, 1)
     V.wait_ge(sem.c_msk, 1)
     for k, d in enumerate(order):
-        V.tensor_scalar(T.rr[:, 8 * k:8 * k + 8], T.msk[:, :], T.lf[:, d:d + 1], None,
+        V.tensor_scalar(T.rr[:, 8 * k:8 * k + 8], T.msk[:, :], T.xs[:, 2 * W + d:2 * W + d + 1], None,
                         AluOpType.mult).then_inc(sem.c_rr, 1)
+    V.memset(T.win2[64:128, :], 0.0).then_inc(sem.c_win2, 1)
 
     PE.wait_ge(sem.x_in, 16)
     PE.wait_ge(sem.c_id, 1)
     PE.transpose(T.pxa[0:W, 0:128], T.xs[:, 0:W], T.ident[:, :]).then_inc(sem.p_t0, 1)
     PE.transpose(T.pxb[0:W, 0:128], T.xs[:, W:2 * W], T.ident[:, :]).then_inc(sem.p_t1, 1)
-    PE.wait_ge(sem.c_rr, N)
+    PE.wait_ge(sem.c_rr, NJ)
     PE.wait_ge(sem.c_sel, 1)
-    PE.matmul(T.po[:, 0:8 * N], T.sel[:, :], T.rr[:, :], True, True).then_inc(sem.p_off, 1)
+    PE.matmul(T.po[:, 0:8 * NJ], T.sel[:, :], T.rr[:, :], True, True).then_inc(sem.p_off, 1)
 
     V.wait_ge(sem.p_t0, 1)
-    V.tensor_copy(T.win[0:W, 0:256:2], T.pxa[0:W, 0:128]).then_inc(sem.c_w, 1)
-    V.wait_ge(sem.p_t1, 1)
-    V.tensor_copy(T.win[0:W, 1:256:2], T.pxb[0:W, 0:128]).then_inc(sem.c_w, 1)
+    copy(V, T.win[0:W, 0:256:2], T.pxa[0:W, 0:128]).then_inc(sem.c_w0, 1)
+    SC.wait_ge(sem.p_t1, 1)
+    copy(SC, T.win[0:W, 1:256:2], T.pxb[0:W, 0:128]).then_inc(sem.c_w1, 1)
     V.wait_ge(sem.p_off, 1)
-    V.tensor_copy(T.off[:, :], T.po[:, 0:8 * N]).then_inc(sem.c_off, 1)
-    V.wait_ge(sem.c_w, 2)
-    V.wait_ge(sem.c_off, 1)
-    V.wait_ge(sem.c_win, 1)
+    V.tensor_copy(T.off[:, :], T.po[:, 0:8 * NJ]).then_inc(sem.c_off, 1)
+    for q in (V, SC):
+        q.wait_ge(sem.c_w0, 1)
+        q.wait_ge(sem.c_w1, 1)
+        q.wait_ge(sem.c_off, 1)
+        q.wait_ge(sem.c_win, 1)
 
-    def gather(k):
-        V.tensor_copy(T.gat[:, CAP * k:CAP * (k + 1)],
-                      T.win[:, 0:256].indirect(T.off[:, 8 * k:8 * k + 8])).then_inc(sem["gk%d" % k], 1)
+    def gather(q, k, win, off):
+        copy(q, T.gat[:, CAP * k:CAP * (k + 1)], win[:, 0:256].indirect(off)).then_inc(sem["gk%d" % k], 1)
 
-    gather(0)
-    gather(1)
-    for k in range(N):
-        bank = T["pb%d" % (k % NB)]
+    def back(k):
         PE.wait_ge(sem["gk%d" % k], 1)
         if k >= NB:
             PE.wait_ge(sem["ck%d" % (k - NB)], 1)
-        PE.transpose(bank[:, 0:W], T.gat[0:W, CAP * k:CAP * (k + 1)], T.ident[0:W, 0:W]).then_inc(sem["bk%d" % k], 1)
-        V.wait_ge(sem["bk%d" % k], 1)
-        V.tensor_copy(T.snd[:, W * k:W * (k + 1)], bank[:, 0:W]).then_inc(sem["ck%d" % k], 1)
-        if k + 2 < N:
-            gather(k + 2)
+        PE.transpose(T["pb%d" % (k % NB)][:, 0:W], T.gat[0:W, CAP * k:CAP * (k + 1)],
+                     T.ident[0:W, 0:W]).then_inc(sem["bk%d" % k], 1)
 
-    sent = 0
-    for s in range(steps):
-        pair = [order[2 * s], order[2 * s + 1]]
-        for d in pair:
-            if not topo.may_write(core, T.cores[d]):
-                raise ValueError("core %d may not write to core %d" % (core, T.cores[d]))
-        eng = engines(topo.mask(core, T.cores[pair[0]]) & topo.mask(core, T.cores[pair[1]]))
-        half = len(eng) // 2
+    def out(q, k):
+        q.wait_ge(sem["bk%d" % k], 1)
+        copy(q, T.snd[:, W * k:W * (k + 1)], T["pb%d" % (k % NB)][:, 0:W]).then_inc(sem["ck%d" % k], 1)
+
+    for q, ks in ((V, list(range(0, NJ, 2))), (SC, list(range(1, NJ, 2)))):
+        gather(q, ks[0], T.win, T.off[:, 8 * ks[0]:8 * ks[0] + 8])
+        for i, k in enumerate(ks):
+            if i + 1 < len(ks):
+                kk = ks[i + 1]
+                gather(q, kk, T.win, T.off[:, 8 * kk:8 * kk + 8])
+            out(q, k)
+    for k in range(NJ):
+        back(k)
+
+    n_raw = len(shares(topo, cores, raw_src, [RAW])[0])
+    V.wait_ge(sem.fa, n_raw)
+    V.tensor_scalar(T.rr2[:, :], T.msk[:, :], T.fx[:, 2 * W + rank:2 * W + rank + 1], None,
+                    AluOpType.mult).then_inc(sem.f_rr, 1)
+    PE.wait_ge(sem.fa, n_raw)
+    PE.wait_ge(sem.c_w0, 1)
+    PE.wait_ge(sem.c_w1, 1)
+    PE.transpose(T.pxa[0:W, 0:128], T.fx[:, 0:W], T.ident[:, :]).then_inc(sem.f_t0, 1)
+    PE.transpose(T.pxb[0:W, 0:128], T.fx[:, W:2 * W], T.ident[:, :]).then_inc(sem.f_t1, 1)
+    PE.wait_ge(sem.f_rr, 1)
+    PE.wait_ge(sem.c_off, 1)
+    PE.matmul(T.po[:, 0:8], T.sel[:, :], T.rr2[:, :], True, True).then_inc(sem.f_po, 1)
+    V.wait_ge(sem.f_t0, 1)
+    copy(V, T.win2[0:W, 0:256:2], T.pxa[0:W, 0:128]).then_inc(sem.f_w0, 1)
+    SC.wait_ge(sem.f_t1, 1)
+    copy(SC, T.win2[0:W, 1:256:2], T.pxb[0:W, 0:128]).then_inc(sem.f_w1, 1)
+    V.wait_ge(sem.f_po, 1)
+    V.tensor_copy(T.off2[:, :], T.po[:, 0:8]).then_inc(sem.f_off, 1)
+    V.wait_ge(sem.f_w0, 1)
+    V.wait_ge(sem.f_w1, 1)
+    V.wait_ge(sem.f_off, 1)
+    V.wait_ge(sem.c_win2, 1)
+    gather(V, NJ, T.win2, T.off2[:, :])
+    back(NJ)
+    out(V, NJ)
+
+    k = 0
+    for call in CALLS:
         trs = []
-        for i, d in enumerate(pair):
-            rid, pid, _se = topo.addr(T.cores[d])
-            k = 2 * s + i
+        for sh, eng in zip(call, shares(topo, cores, rank, call)):
+            rid, pid, _se = topo.addr(cores[(rank + sh) % N])
             g.wait_ge(sem["ck%d" % k], 1)
             trs.append(RemoteDMATransfer(dst_ids=[DstId(rid=rid, pnc=pid)],
-                                         dma_engine_mask=sum(1 << e for e in eng[i * half:(i + 1) * half]),
-                                         remote_sem=sem["a%d" % rank],
+                                         dma_engine_mask=sum(1 << e for e in eng), remote_sem=sem["a%d" % rank],
                                          src=T.snd[:, W * k:W * (k + 1)], dst=T.land[rank]))
-            sent += half
+            sent += len(eng)
+            k += 1
         g.remote_dma_fused(trs, local_sem=sem.sent)
 
-    SY.wait_ge(sem["ck%d" % (N - 1)], 1)
-    SY.dma_start(T.y[CAP * rank:CAP * (rank + 1), :], T.snd[:, W * (N - 1):W * N]).then_inc(sem.st, 16)
-    for s in range(steps):
-        for q, src in ((SY, down[s]), (SC, up[s])):
-            other = (2 * src - rank) % N
-            n = len(engines(topo.mask(T.cores[src], core) & topo.mask(T.cores[src], T.cores[other]))) // 2
-            q.wait_ge(sem["a%d" % src], n)
-            q.dma_start(T.y[CAP * src:CAP * (src + 1), :], T.land[src]).then_inc(sem.st, 16)
+    def from_snd(q, k, src):
+        q.wait_ge(sem["ck%d" % k], 1)
+        q.dma_start(T.y[CAP * src:CAP * (src + 1), :], T.snd[:, W * k:W * (k + 1)]).then_inc(sem.st, 16)
+
+    from_snd(SY, NJ - 1, rank)
+    for call in CALLS:
+        for i, sh in enumerate(call):
+            src = (rank - sh) % N
+            SY.wait_ge(sem["a%d" % src], len(shares(topo, cores, src, call)[i]))
+            SY.dma_start(T.y[CAP * src:CAP * (src + 1), :], T.land[src]).then_inc(sem.st, 16)
+    from_snd(SC, NJ, raw_src)
 
     g.wait_ge(sem.sent, sent)
     g.wait_ge(sem.st, 16 * N)

from concourse.bass import DstId, RemoteDMATransfer
from concourse.mybir import AluOpType, ActivationFunctionType

N = 7
CAP = 128
W = 64
NB = 4
NJ = N - 1
XW = 2 * W + N

SCRATCH = {
    "li": ("sbuf", [128, N], "int32"),
    "xs": ("sbuf", [128, XW], "float32"),
    "fx": ("sbuf", [128, XW], "float32"),
    "tt": ("sbuf", [128, 128], "int32"),
    "m1": ("sbuf", [128, 8], "int32"),
    "msk": ("sbuf", [128, 8], "float32"),
    "s1": ("sbuf", [128, 128], "int32"),
    "sel": ("sbuf", [128, 128], "bfloat16"),
    "ident": ("sbuf", [128, 128], "float32"),
    "rr": ("sbuf", [128, 8 * NJ], "bfloat16"),
    "rr2": ("sbuf", [128, 8], "bfloat16"),
    "off": ("sbuf", [128, 8 * NJ], "uint16"),
    "off2": ("sbuf", [128, 8], "uint16"),
    "win": ("sbuf", [128, 256], "float32"),
    "win2": ("sbuf", [128, 256], "float32"),
    "gat": ("sbuf", [128, N * CAP], "float32"),
    "snd": ("sbuf", [128, N * W], "float32"),
    "land": ("dram", [N, 128, W], "float32"),
    "pxa": ("psum", [128, 512], "float32"),
    "pxb": ("psum", [128, 512], "float32"),
    "po": ("psum", [128, 512], "float32"),
    "pb0": ("psum", [128, 512], "float32"),
    "pb1": ("psum", [128, 512], "float32"),
    "pb2": ("psum", [128, 512], "float32"),
    "pb3": ("psum", [128, 512], "float32"),
}
SEMAPHORES = (["l_in", "x_in", "c_t", "c_win", "c_win2", "c_m1", "c_id", "c_s1", "c_msk", "c_sel", "c_lf", "c_rr",
               "c_w0", "c_w1", "c_off", "p_t0", "p_t1", "p_off", "sent", "st",
               "fa", "f_rr", "f_t0", "f_t1", "f_po", "f_w0", "f_w1", "f_off"]
              + ["gk%d" % k for k in range(N)] + ["bk%d" % k for k in range(N)] + ["ck%d" % k for k in range(N)]
              + ["a%d" % k for k in range(N)])

CALLS = [[2, -2], [3, -3], [-1]]
RAW = 1


def engines(m):
    return [e for e in range(m.bit_length()) if (m >> e) & 1]


def shares(topo, cores, src, call):
    m = None
    for sh in call:
        mm = topo.mask(cores[src], cores[(src + sh) % N])
        m = mm if m is None else (m & mm)
    eng = engines(m)
    part = len(eng) // len(call)
    return [eng[i * part:(i + 1) * part] for i in range(len(call))]


def rank_program(g, core, T, topo):
    rank = T.rank_of(core)
    if rank is None:
        return
    V, PE, SY, SC, sem = g.vector, g.tensor, g.sync, g.scalar, T.sem
    cores = T.cores
    order = [(rank + sh) % N for call in CALLS for sh in call] + [rank]
    raw_dst, raw_src = (rank + RAW) % N, (rank - RAW) % N
    for d in order[:-1] + [raw_dst]:
        if not topo.may_write(core, cores[d]):
            raise ValueError("core %d may not write to core %d" % (core, cores[d]))

    def copy(q, out, in_):
        if q is V:
            return V.tensor_copy(out, in_)
        return SC.activation(out, in_, ActivationFunctionType.Copy)

    SY.dma_start(T.li[:, :], T.l[:, :]).then_inc(sem.l_in, 16)
    SC.dma_start(T.xs[:, 0:2 * W], T.x[:, :]).then_inc(sem.x_in, 16)

    g.iota(T.tt[:, :], [[-1, 128]], 128, 1).then_inc(sem.c_t, 1)
    V.memset(T.win[64:128, :], 0.0).then_inc(sem.c_win, 1)
    V.wait_ge(sem.c_t, 1)
    V.tensor_scalar(T.ident[:, :], T.tt[:, :], 128, None, AluOpType.is_equal).then_inc(sem.c_id, 1)
    V.tensor_scalar(T.m1[:, :], T.tt[:, 0:128:16], 4, None, AluOpType.arith_shift_right).then_inc(sem.c_m1, 1)
    V.wait_ge(sem.c_m1, 1)
    V.tensor_scalar(T.msk[:, :], T.m1[:, :], 8, None, AluOpType.is_equal).then_inc(sem.c_msk, 1)
    V.wait_ge(sem.l_in, 16)
    V.tensor_copy(T.xs[:, 2 * W:XW], T.li[:, :]).then_inc(sem.c_lf, 1)

    sent = 0
    raw_eng = shares(topo, cores, rank, [RAW])[0]
    rid, pid, _se = topo.addr(cores[raw_dst])
    g.wait_ge(sem.x_in, 16)
    g.wait_ge(sem.c_lf, 1)
    g.remote_dma_fused([RemoteDMATransfer(dst_ids=[DstId(rid=rid, pnc=pid)],
                                          dma_engine_mask=sum(1 << e for e in raw_eng), remote_sem=sem.fa,
                                          src=T.xs[:, :], dst=T.fx[:, :])], local_sem=sem.sent)
    sent += len(raw_eng)

    V.tensor_scalar(T.s1[:, :], T.tt[:, :], 15, None, AluOpType.bitwise_and).then_inc(sem.c_s1, 1)
    V.wait_ge(sem.c_s1, 1)
    V.tensor_scalar(T.sel[:, :], T.s1[:, :], 0, None, AluOpType.is_equal).then_inc(sem.c_sel, 1)
    V.wait_ge(sem.c_lf, 1)
    V.wait_ge(sem.c_msk, 1)
    for k, d in enumerate(order):
        V.tensor_scalar(T.rr[:, 8 * k:8 * k + 8], T.msk[:, :], T.xs[:, 2 * W + d:2 * W + d + 1], None,
                        AluOpType.mult).then_inc(sem.c_rr, 1)
    V.memset(T.win2[64:128, :], 0.0).then_inc(sem.c_win2, 1)

    PE.wait_ge(sem.x_in, 16)
    PE.wait_ge(sem.c_id, 1)
    PE.transpose(T.pxa[0:W, 0:128], T.xs[:, 0:W], T.ident[:, :]).then_inc(sem.p_t0, 1)
    PE.transpose(T.pxb[0:W, 0:128], T.xs[:, W:2 * W], T.ident[:, :]).then_inc(sem.p_t1, 1)
    PE.wait_ge(sem.c_rr, NJ)
    PE.wait_ge(sem.c_sel, 1)
    PE.matmul(T.po[:, 0:8 * NJ], T.sel[:, :], T.rr[:, :], True, True).then_inc(sem.p_off, 1)

    V.wait_ge(sem.p_t0, 1)
    copy(V, T.win[0:W, 0:256:2], T.pxa[0:W, 0:128]).then_inc(sem.c_w0, 1)
    SC.wait_ge(sem.p_t1, 1)
    copy(SC, T.win[0:W, 1:256:2], T.pxb[0:W, 0:128]).then_inc(sem.c_w1, 1)
    V.wait_ge(sem.p_off, 1)
    V.tensor_copy(T.off[:, :], T.po[:, 0:8 * NJ]).then_inc(sem.c_off, 1)
    for q in (V, SC):
        q.wait_ge(sem.c_w0, 1)
        q.wait_ge(sem.c_w1, 1)
        q.wait_ge(sem.c_off, 1)
        q.wait_ge(sem.c_win, 1)

    def gather(q, k, win, off):
        copy(q, T.gat[:, CAP * k:CAP * (k + 1)], win[:, 0:256].indirect(off)).then_inc(sem["gk%d" % k], 1)

    def back(k):
        PE.wait_ge(sem["gk%d" % k], 1)
        if k >= NB:
            PE.wait_ge(sem["ck%d" % (k - NB)], 1)
        PE.transpose(T["pb%d" % (k % NB)][:, 0:W], T.gat[0:W, CAP * k:CAP * (k + 1)],
                     T.ident[0:W, 0:W]).then_inc(sem["bk%d" % k], 1)

    def out(q, k):
        q.wait_ge(sem["bk%d" % k], 1)
        copy(q, T.snd[:, W * k:W * (k + 1)], T["pb%d" % (k % NB)][:, 0:W]).then_inc(sem["ck%d" % k], 1)

    for q, ks in ((V, list(range(0, NJ, 2))), (SC, list(range(1, NJ, 2)))):
        gather(q, ks[0], T.win, T.off[:, 8 * ks[0]:8 * ks[0] + 8])
        for i, k in enumerate(ks):
            if i + 1 < len(ks):
                kk = ks[i + 1]
                gather(q, kk, T.win, T.off[:, 8 * kk:8 * kk + 8])
            out(q, k)
    for k in range(NJ):
        back(k)

    n_raw = len(shares(topo, cores, raw_src, [RAW])[0])
    V.wait_ge(sem.fa, n_raw)
    V.tensor_scalar(T.rr2[:, :], T.msk[:, :], T.fx[:, 2 * W + rank:2 * W + rank + 1], None,
                    AluOpType.mult).then_inc(sem.f_rr, 1)
    PE.wait_ge(sem.fa, n_raw)
    PE.wait_ge(sem.c_w0, 1)
    PE.wait_ge(sem.c_w1, 1)
    PE.transpose(T.pxa[0:W, 0:128], T.fx[:, 0:W], T.ident[:, :]).then_inc(sem.f_t0, 1)
    PE.transpose(T.pxb[0:W, 0:128], T.fx[:, W:2 * W], T.ident[:, :]).then_inc(sem.f_t1, 1)
    PE.wait_ge(sem.f_rr, 1)
    PE.wait_ge(sem.c_off, 1)
    PE.matmul(T.po[:, 0:8], T.sel[:, :], T.rr2[:, :], True, True).then_inc(sem.f_po, 1)
    V.wait_ge(sem.f_t0, 1)
    copy(V, T.win2[0:W, 0:256:2], T.pxa[0:W, 0:128]).then_inc(sem.f_w0, 1)
    SC.wait_ge(sem.f_t1, 1)
    copy(SC, T.win2[0:W, 1:256:2], T.pxb[0:W, 0:128]).then_inc(sem.f_w1, 1)
    V.wait_ge(sem.f_po, 1)
    V.tensor_copy(T.off2[:, :], T.po[:, 0:8]).then_inc(sem.f_off, 1)
    V.wait_ge(sem.f_w0, 1)
    V.wait_ge(sem.f_w1, 1)
    V.wait_ge(sem.f_off, 1)
    V.wait_ge(sem.c_win2, 1)
    gather(V, NJ, T.win2, T.off2[:, :])
    back(NJ)
    out(V, NJ)

    k = 0
    for call in CALLS:
        trs = []
        for sh, eng in zip(call, shares(topo, cores, rank, call)):
            rid, pid, _se = topo.addr(cores[(rank + sh) % N])
            g.wait_ge(sem["ck%d" % k], 1)
            trs.append(RemoteDMATransfer(dst_ids=[DstId(rid=rid, pnc=pid)],
                                         dma_engine_mask=sum(1 << e for e in eng), remote_sem=sem["a%d" % rank],
                                         src=T.snd[:, W * k:W * (k + 1)], dst=T.land[rank]))
            sent += len(eng)
            k += 1
        g.remote_dma_fused(trs, local_sem=sem.sent)

    def from_snd(q, k, src):
        q.wait_ge(sem["ck%d" % k], 1)
        q.dma_start(T.y[CAP * src:CAP * (src + 1), :], T.snd[:, W * k:W * (k + 1)]).then_inc(sem.st, 16)

    from_snd(SY, NJ - 1, rank)
    for call in CALLS:
        for i, sh in enumerate(call):
            src = (rank - sh) % N
            SY.wait_ge(sem["a%d" % src], len(shares(topo, cores, src, call)[i]))
            SY.dma_start(T.y[CAP * src:CAP * (src + 1), :], T.land[src]).then_inc(sem.st, 16)
    from_snd(SC, NJ, raw_src)

    g.wait_ge(sem.sent, sent)
    g.wait_ge(sem.st, 16 * N)
